import numpy as np
import ml_dtypes


def mxq(x, axis, fmt="e4m3"):
    dtype, down = {"e4m3": (ml_dtypes.float8_e4m3fn, 7), "e5m2": (ml_dtypes.float8_e5m2, 14)}[fmt]
    v = np.moveaxis(np.asarray(x, np.float32).astype(ml_dtypes.bfloat16).astype(np.float64), axis, -1)
    blocks = v.reshape(v.shape[:-1] + (-1, 32))
    amax = np.abs(blocks).max(-1, keepdims=True)
    byte = np.maximum(np.where(amax > 0, np.frexp(amax)[1] - 1 + 127, 0) - down, 1)
    scale = np.exp2(byte - 127.0)
    codes = (blocks / scale).astype(np.float32).astype(dtype).astype(np.float64)
    return np.moveaxis((codes * scale).reshape(v.shape), -1, axis)


WIDE = False


def mx_kscale(k):
    if not WIDE:
        return np.ones(k)
    levels = np.array([10, -10, 5, -5, 0])
    if k % 512:
        return np.exp2(np.random.permutation(np.resize(levels, k // 32))).repeat(32)
    a = np.empty((k // 512, 16))
    for p in range(k // 512):
        a[p, :8] = np.random.permutation(np.resize(levels, 8))
        for g in range(8):
            far = levels[np.abs(levels - a[p, g]) >= 10]
            a[p, g + 8] = far[np.random.randint(len(far))]
    return np.exp2(a.ravel()).repeat(32)


BF16 = ml_dtypes.bfloat16


def bf(x):
    return np.asarray(x, np.float32).astype(BF16)


def f64(x):
    return np.asarray(x).astype(np.float64)


E2M1 = np.array([0.0, 0.5, 1.0, 1.5, 2.0, 3.0, 4.0, 6.0, -0.0, -0.5, -1.0, -1.5, -2.0, -3.0, -4.0, -6.0])


def pack_weight(w, fmt):
    k, n = w.shape
    w = f64(bf(w)).reshape(k // 32, 32, n)
    amax = np.abs(w).max(1)
    if fmt == "e4m3":
        byte = np.frexp(amax)[1] - 1 + 127 - 7
    else:
        mant, ex = np.frexp(amax / 6.0)
        byte = np.where(mant > 0.5, ex, ex - 1) + 127
    byte = np.clip(np.where(amax > 0, byte, 1), 1, 254)
    scaled = (w * np.exp2(127.0 - byte)[:, None, :]).reshape(k, n).astype(np.float32)
    by_word = np.ascontiguousarray(scaled.reshape(k // 512, 128, 4, n).transpose(0, 1, 3, 2))
    if fmt == "e4m3":
        words = by_word.astype(ml_dtypes.float8_e4m3fn).view(np.uint8)
    else:
        c = by_word.astype(ml_dtypes.float4_e2m1fn).view(np.uint8) & 0xF
        words = c[..., 0::2] | (c[..., 1::2] << 4)
    return np.ascontiguousarray(words), np.ascontiguousarray(byte.astype(np.uint8).reshape(k // 512, 16, n))


def unpack_weight(words, scales, fmt):
    g, p, n, _ = words.shape
    if fmt == "e4m3":
        vals = np.ascontiguousarray(words).view(ml_dtypes.float8_e4m3fn).astype(np.float64)
    else:
        nib = np.empty((g, p, n, 4), np.uint8)
        nib[..., 0::2] = words & 0xF
        nib[..., 1::2] = words >> 4
        vals = E2M1[nib]
    vals = vals * np.repeat(np.exp2(scales.astype(np.float64) - 127.0), 8, axis=1)[..., None]
    return vals.transpose(0, 1, 3, 2).reshape(g * 512, n)
def pack4(w):
    words, scales = pack_weight(w, "e2m1")
    return words.reshape(words.shape[0], 128, -1), scales


def unpack4(words, scales):
    return unpack_weight(words.reshape(words.shape[0], 128, -1, 2), scales, "e2m1")


M, KO, KR, F, N = 1024, 512, 1024, 2048, 512


def draw0():
    so, sr = mx_kscale(KO), mx_kscale(KR)
    t = mx_kscale(F)
    er = np.random.standard_normal((KR, F)) / np.sqrt(KO + KR) / sr[:, None] * t
    d = np.random.standard_normal((F, N)) / np.sqrt(F) / t[:, None]
    er_words, er_scales = pack4(er)
    d_words, d_scales = pack4(d)
    return {
        "xo": bf(2.0 * np.random.standard_normal((M, KO)) * so),
        "xr": bf(np.random.standard_normal((M, KR)) * sr),
        "eo": bf(np.random.standard_normal((KO, F)) / np.sqrt(KO + KR) / so[:, None] * t),
        "er_words": er_words,
        "er_scales": er_scales,
        "b": bf(0.5 * np.random.standard_normal(F) * t),
        "d_words": d_words,
        "d_scales": d_scales,
        "b_read": bf(0.3 * np.random.standard_normal(N)),
        "r": bf(np.exp(0.3 * np.random.standard_normal(M))),
    }


def core(xo, xr, eo, er_words, er_scales, b, d_words, d_scales, b_read, r):
    outlier = mxq(f64(xo), 1, "e4m3") @ mxq(f64(eo), 0, "e4m3")
    rest = mxq(f64(xr), 1, "e4m3") @ unpack4(er_words, er_scales)
    c = np.maximum(outlier + rest + f64(b), 0.0)
    y = mxq(c, 1, "e4m3") @ unpack4(d_words, d_scales)
    return (y + f64(b_read)) * f64(r)[:, None]


def e4m3fn_bytes(y):
    return np.clip(np.asarray(y, np.float64), -448.0, 448.0).astype(np.float32).astype(ml_dtypes.float8_e4m3fn).view(np.uint8)


def e4m3fn_values(b):
    return np.asarray(b, np.uint8).view(ml_dtypes.float8_e4m3fn).astype(np.float64)


def setup_inputs():
    d = draw0()
    x0 = np.asarray(d['xr']).astype(np.float64)
    s = (np.max(np.abs(x0), axis=(0,), keepdims=True) / 448.0).astype(np.float32)
    out = {}
    for k, v in d.items():
        if k == 'xr':
            out['xr_bytes'] = e4m3fn_bytes(x0 / s.astype(np.float64))
            out['xr_scale'] = s
        else:
            out[k] = v
    return out


def reference(xo, xr_bytes, xr_scale, eo, er_words, er_scales, b, d_words, d_scales, b_read, r):
    return core(xo, e4m3fn_values(xr_bytes) * xr_scale.astype(np.float64), eo, er_words, er_scales, b, d_words, d_scales, b_read, r)

@@ -1,0 +1,416 @@
+from contextlib import ExitStack
+
+import concourse.mybir as mybir
+from concourse.masks import make_identity
+
+M, KO, KR, F, N = 1024, 512, 1024, 2048, 512
+FLOPS = 2 * M * F * (KO + KR) + 2 * M * F * N
+
+F32 = mybir.dt.float32
+BF16 = mybir.dt.bfloat16
+I32 = mybir.dt.int32
+U32 = mybir.dt.uint32
+U8 = mybir.dt.uint8
+E4 = mybir.dt.float8_e4m3fn_x4
+E2 = mybir.dt.float4_e2m1fn_x4
+FP8 = mybir.dt.float8_e4m3fn
+ACT = mybir.ActivationFunctionType
+ALU = mybir.AluOpType
+
+P = 128
+
+
+def tile_relu_dictionary_readout_s3_kernel(
+    tc, xo, xr_bytes, xr_scale, eo, er_words, er_scales, b, d_words, d_scales, b_read, r, out
+):
+    nc = tc.nc
+    with ExitStack() as ctx:
+        keep = ctx.enter_context(tc.tile_pool(name="keep", bufs=1))
+        roll = ctx.enter_context(tc.tile_pool(name="roll", bufs=4))
+        psum = ctx.enter_context(tc.psum_pool(name="psum", bufs=1))
+        ctx.enter_context(tc.manual_schedule())
+
+        def kt(shape, dt, name):
+            return keep.tile(shape, dt, name=name, tag=name, align_bytes=64)
+
+        ident = kt([P, P], F32, "ident")
+        er_sc_raw = kt([P, 2, F], U8, "er_sc_raw")
+        d_sc = kt([P, 4, N], U8, "d_sc")
+        warm = kt([P, 1], F32, "warm")
+        xr_raw = [kt([P, 4, KR], U8, "xr_raw%d" % h) for h in range(2)]
+        xr_wide = kt([P, 8, KR], BF16, "xr_wide")
+        xo_raw = [kt([P, 4, KO], BF16, "xo_raw%d" % h) for h in range(2)]
+        xr_sc = kt([P, 2, 4], F32, "xr_sc")
+        x_in = [[kt([P, 512, 4], BF16, "x_in%d_%d" % (h, c)) for c in range(3)] for h in range(2)]
+        x_codes = [[kt([P, 512], U32, "x_codes%d_%d" % (h, c)) for c in range(3)] for h in range(2)]
+        x_scales = [[kt([P, 512], U8, "x_scales%d_%d" % (h, c)) for c in range(3)] for h in range(2)]
+        eo_raw = [kt([P, 4, 512], BF16, "eo_raw%d" % a) for a in range(4)]
+        eo_in = [kt([P, 2048], BF16, "eo_in%d" % a) for a in range(4)]
+        eo_codes = [kt([P, 512], U32, "eo_codes%d" % a) for a in range(4)]
+        eo_scales = [kt([P, 512], U8, "eo_scales%d" % a) for a in range(4)]
+        er_raw = [kt([P, 2, 1024], U8, "er_raw%d" % a) for a in range(4)]
+        er_codes = [kt([P, 2, 1024], U8, "er_codes%d" % a) for a in range(4)]
+        er_sc = [kt([P, 2, 512], U8, "er_sc%d" % a) for a in range(4)]
+        d_codes = kt([P, 4, 2 * N], U8, "d_codes")
+        c_codes = [[kt([P, 512], U32, "c_codes%d_%d" % (a, h)) for h in range(2)] for a in range(4)]
+        c_scales = [[kt([P, 512], U8, "c_scales%d_%d" % (a, h)) for h in range(2)] for a in range(4)]
+        b_bf = kt([P, 4, 4], BF16, "b_bf")
+        b_f = kt([P, 16], F32, "b_f")
+        r_bf = kt([P, 8], BF16, "r_bf")
+        r_f = kt([P, 8], F32, "r_f")
+        br_bf = kt([P, N], BF16, "br_bf")
+        rb = kt([P, 8, N], F32, "rb")
+
+        xo_v = xo.rearrange("(p i) k -> p i k", i=8)
+        xr_v = xr_bytes.rearrange("(p i) k -> p i k", i=8)
+        eo_v = eo.rearrange("(p j) f -> p j f", j=4)
+        er_v = er_words.rearrange("g p n -> p g n")
+        out_v = out.rearrange("(p i) n -> p i n", i=8)
+
+        nc.vector.memset(warm[:], 0.0)
+        make_identity(nc, ident[:])
+        nc.gpsimd.memset(er_sc_raw[:].rearrange("p g n -> p (g n)").bitcast(I32), 0)
+        nc.gpsimd.memset(d_sc[:].rearrange("p g n -> p (g n)").bitcast(I32), 0)
+
+        nc.scalar.dma_start(out=xr_sc[:], in_=xr_scale.rearrange("o (g p t) -> p (o g) t", p=128, t=4))
+        nc.scalar.dma_start(out=b_bf[:], in_=b.rearrange("(a p t) -> p a t", p=128, t=4))
+        nc.scalar.dma_start(out=r_bf[:], in_=r.rearrange("(p i) -> p i", i=8))
+        nc.scalar.activation(out=warm[:], in_=warm[:], func=ACT.Relu)
+
+        def load_xr(h, lo, hi):
+            nc.sync.dma_start(out=xr_raw[h][:, lo:hi, :], in_=xr_v[:, 4 * h + lo : 4 * h + hi, :])
+
+        def load_xo(h):
+            nc.sync.dma_start(out=xo_raw[h][:], in_=xo_v[:, 4 * h : 4 * h + 4, :])
+
+        def load_eo(a):
+            nc.sync.dma_start(out=eo_raw[a][:], in_=eo_v[:, :, 512 * a : 512 * a + 512])
+
+        def load_er(a):
+            nc.sync.dma_start(out=er_raw[a][:], in_=er_v[:, :, 1024 * a : 1024 * a + 1024])
+
+        load_xr(0, 0, 1)
+        load_xr(0, 1, 2)
+        load_er(0)
+        load_xr(0, 2, 4)
+        er_sc_v = er_scales.bitcast(I32)
+        for q in range(4):
+            nc.sync.dma_start(
+                out=er_sc_raw[32 * q : 32 * q + 4, :, :].bitcast(I32),
+                in_=er_sc_v[:, 4 * q : 4 * q + 4, :].rearrange("g q n -> q g n"),
+            )
+        load_eo(0)
+        load_xo(0)
+        load_eo(1)
+        load_er(1)
+        load_xr(1, 0, 2)
+        load_xr(1, 2, 4)
+        load_eo(2)
+        load_er(2)
+        load_xo(1)
+        load_eo(3)
+        load_er(3)
+        nc.sync.dma_start(out=d_codes[:], in_=d_words.rearrange("g p n -> p g n"))
+        d_sc_v = d_scales.bitcast(I32)
+        for q in range(4):
+            nc.sync.dma_start(
+                out=d_sc[32 * q : 32 * q + 4, :, :].bitcast(I32),
+                in_=d_sc_v[:, 4 * q : 4 * q + 4, :].rearrange("g q n -> q g n"),
+            )
+        nc.sync.dma_start(out=br_bf[:], in_=b_read.partition_broadcast(P))
+
+        nc.gpsimd.tensor_copy(out=b_f[:], in_=b_bf[:].rearrange("p a t -> p (a t)"))
+        nc.gpsimd.tensor_copy(out=r_f[:], in_=r_bf[:])
+
+        def bank(k, name):
+            return psum.tile([P, 512], F32, name=name, tag="bank%d" % k)
+
+        def widen(i, eng):
+            src = xr_raw[i // 4][:, i % 4, :].bitcast(FP8)
+            if eng == "s":
+                nc.scalar.activation(out=xr_wide[:, i, :], in_=src, func=ACT.Copy)
+            else:
+                nc.vector.tensor_copy(out=xr_wide[:, i, :], in_=src)
+
+        xr_bank = {}
+
+        def xr_turn(i, k):
+            t = bank(k, "xr_t%d" % i)
+            xr_bank[i] = t
+            words = xr_wide[:, i, :].bitcast(F32)
+            for g in range(2):
+                for u in range(2):
+                    c = 128 * (2 * g + u)
+                    nc.tensor.transpose(t[:, c : c + 128], words[:, 256 * g + u : 256 * (g + 1) : 2], ident[:])
+
+        def xr_product(i):
+            h = i // 4
+            cols = slice(128 * (i % 4), 128 * (i % 4) + 128)
+            t = xr_bank[i][:].bitcast(BF16)
+            for g in range(2):
+                nc.vector.tensor_tensor(
+                    out=x_in[h][1 + g][:, cols, :].rearrange("p m (u e) -> p m u e", u=2),
+                    in0=t[:, 512 * g : 512 * (g + 1)].rearrange("p (u m e) -> p m u e", u=2, e=2),
+                    in1=xr_sc[:, g, :].rearrange("p (u e) -> p u e", u=2).unsqueeze(1).to_broadcast([P, 128, 2, 2]),
+                    op=ALU.mult,
+                )
+
+        xo_bank = {}
+
+        def xo_turn(j, k):
+            t = bank(k, "xo_t%d" % j)
+            xo_bank[j] = t
+            for d in range(2):
+                i = 2 * j + d
+                words = xo_raw[i // 4][:, i % 4, :].bitcast(F32)
+                for u in range(2):
+                    c = 128 * (2 * d + u)
+                    nc.tensor.transpose(t[:, c : c + 128], words[:, u:256:2], ident[:])
+
+        def xo_empty(j, eng):
+            h = j // 2
+            dst = x_in[h][0][:, 256 * (j % 2) : 256 * (j % 2) + 256, :].rearrange("p m t -> p (m t)").bitcast(F32)
+            o = dst.rearrange("p (d m u) -> p d m u", d=2, u=2)
+            s = xo_bank[j][:].rearrange("p (d u m) -> p d m u", d=2, u=2)
+            if eng == "s":
+                nc.scalar.copy(out=o, in_=s)
+            else:
+                nc.vector.tensor_copy(out=o, in_=s)
+
+        def x_quant(h, c):
+            nc.vector.quantize_mx(
+                out=x_codes[h][c][:].bitcast(E4), scales=x_scales[h][c][:], in_=x_in[h][c][:].rearrange("p m t -> p (m t)")
+            )
+
+        def eo_lay(a, eng):
+            o = eo_in[a][:].rearrange("p (t m j) -> p t m j", t=4, j=4)
+            s = eo_raw[a][:].rearrange("p j (m t) -> p t m j", t=4)
+            if eng == "s":
+                nc.scalar.copy(out=o, in_=s)
+            elif eng == "g":
+                nc.gpsimd.tensor_scalar(out=o, in0=s, scalar1=1.0, scalar2=0.0, op0=ALU.mult, op1=ALU.add)
+            else:
+                nc.vector.tensor_copy(out=o, in_=s)
+
+        def eo_quant(a):
+            nc.vector.quantize_mx(out=eo_codes[a][:].bitcast(E4), scales=eo_scales[a][:], in_=eo_in[a][:])
+
+        def er_move(a):
+            for g in range(2):
+                nc.vector.tensor_copy(
+                    out=er_codes[a][:, g, :].rearrange("p (t m c) -> p t m c", t=4, c=2),
+                    in_=er_raw[a][:, g, :].rearrange("p (m t c) -> p t m c", t=4, c=2),
+                )
+
+        def er_move_scales(a):
+            nc.vector.tensor_copy(
+                out=er_sc[a][:].rearrange("p g (t m) -> p g t m", t=4),
+                in_=er_sc_raw[:, :, 512 * a : 512 * a + 512].rearrange("p g (m t) -> p g t m", t=4),
+            )
+
+        s1_bank = {}
+
+        def s1(a, h, t, c, first=0, last=2):
+            if c == first:
+                s1_bank[a, h, t] = bank(t, "s1_%d_%d_%d" % (a, h, t))
+            acc = s1_bank[a, h, t]
+            cols = slice(128 * t, 128 * t + 128)
+            if c == 0:
+                w, ws = eo_codes[a][:, cols].bitcast(E4), eo_scales[a][:, cols]
+            else:
+                w, ws = er_codes[a][:, c - 1, 256 * t : 256 * t + 256].bitcast(E2), er_sc[a][:, c - 1, cols]
+            nc.tensor.matmul_mx(
+                out=acc[:],
+                lhsT=w,
+                lhsT_scale=ws,
+                rhs=x_codes[h][c][:].bitcast(E4),
+                rhs_scale=x_scales[h][c][:],
+                start=(c == first),
+                stop=(c == last),
+            )
+
+        c_act = {}
+
+        def empty(a, h, t, eng):
+            if t == 0:
+                c_act[a, h] = roll.tile([P, 4, 512], BF16, name="c_act", tag="c_act", align_bytes=64)
+            o = c_act[a, h][:, t, :]
+            s = s1_bank[a, h, t][:]
+            bias = b_f[:, 4 * a + t : 4 * a + t + 1]
+            if eng == "s":
+                nc.scalar.activation(out=o, in_=s, func=ACT.Relu, bias=bias)
+            else:
+                nc.vector.tensor_scalar(out=o, in0=s, scalar1=bias, scalar2=0.0, op0=ALU.add, op1=ALU.max)
+
+        c_in = {}
+
+        def c_lay(a, h, lo, hi, eng):
+            if lo == 0:
+                c_in[a, h] = roll.tile([P, 512, 4], BF16, name="c_in", tag="c_in", align_bytes=64)
+            o = c_in[a, h][:, lo:hi, :]
+            s = c_act[a, h][:, :, lo:hi].rearrange("p t m -> p m t")
+            if eng == "s":
+                nc.scalar.copy(out=o, in_=s)
+            else:
+                nc.vector.tensor_copy(out=o, in_=s)
+
+        def c_quant(a, h, lo, hi):
+            nc.vector.quantize_mx(
+                out=c_codes[a][h][:, lo:hi].bitcast(E4),
+                scales=c_scales[a][h][:, lo:hi],
+                in_=c_in[a, h][:, lo:hi, :].rearrange("p m t -> p (m t)"),
+            )
+
+        s2_bank = {}
+
+        def s2(i, a, k):
+            if a == 0:
+                s2_bank[i] = bank(k, "s2_%d" % i)
+            h = i // 4
+            cols = slice(128 * (i % 4), 128 * (i % 4) + 128)
+            nc.tensor.matmul_mx(
+                out=s2_bank[i][:],
+                lhsT=c_codes[a][h][:, cols].bitcast(E4),
+                lhsT_scale=c_scales[a][h][:, cols],
+                rhs=d_codes[:, a, :].bitcast(E2),
+                rhs_scale=d_sc[:, a, :],
+                start=(a == 0),
+                stop=(a == 3),
+            )
+
+        def finish(i):
+            y = roll.tile([P, N], F32, name="y", tag="y", align_bytes=64)
+            nc.vector.scalar_tensor_tensor(
+                out=y[:], in0=s2_bank[i][:], scalar=r_f[:, i : i + 1], in1=rb[:, i, :], op0=ALU.mult, op1=ALU.add
+            )
+            nc.sync.dma_start(out=out_v[:, i, :], in_=y[:])
+
+
+        def stage1(a, h, ts=(0, 1, 2, 3)):
+            for t in ts:
+                for c in range(3):
+                    s1(a, h, t, c)
+
+        def drain(a, h):
+            for t in range(4):
+                empty(a, h, t, "s")
+
+        def lay(a, h, split):
+            if split > 0:
+                c_lay(a, h, 0, split, "v")
+            if split < 512:
+                c_lay(a, h, split, 512, "s")
+
+        def quant(a, h):
+            c_quant(a, h, 0, 512)
+
+        widen(0, "s")
+        widen(1, "v")
+        widen(2, "s")
+        widen(3, "s")
+        er_move(0)
+        for i in range(4):
+            xr_turn(i, 4 + i)
+        xo_turn(0, 4)
+        xo_turn(1, 5)
+        eo_lay(0, "g")
+        for i in range(4):
+            xr_product(i)
+        xo_empty(0, "s")
+        xo_empty(1, "s")
+        er_move_scales(0)
+        x_quant(0, 1)
+        x_quant(0, 2)
+        for t in range(4):
+            s1(0, 0, t, 1, 1, 0)
+            s1(0, 0, t, 2, 1, 0)
+        x_quant(0, 0)
+        eo_quant(0)
+        for t in range(4):
+            s1(0, 0, t, 0, 1, 0)
+        eo_lay(1, "g")
+        widen(4, "s")
+        widen(5, "s")
+        xr_turn(4, 4)
+        eo_quant(1)
+        er_move(1)
+        er_move_scales(1)
+        eo_lay(2, "g")
+        drain(0, 0)
+        stage1(1, 0)
+        xr_turn(5, 5)
+        widen(6, "s")
+        widen(7, "s")
+        xr_product(4)
+        eo_quant(2)
+        er_move(2)
+        er_move_scales(2)
+        drain(1, 0)
+        xr_product(5)
+        stage1(2, 0, (0, 1))
+        xr_turn(6, 6)
+        xr_turn(7, 7)
+        stage1(2, 0, (2,))
+        xo_turn(2, 4)
+        xo_turn(3, 5)
+        stage1(2, 0, (3,))
+        xr_product(6)
+        xr_product(7)
+        xo_empty(2, "s")
+        xo_empty(3, "s")
+        drain(2, 0)
+        x_quant(1, 1)
+        x_quant(1, 2)
+        x_quant(1, 0)
+        eo_lay(3, "s")
+        lay(0, 0, 512)
+        stage1(0, 1)
+        eo_quant(3)
+        er_move(3)
+        er_move_scales(3)
+        quant(0, 0)
+        stage1(1, 1)
+        drain(0, 1)
+        lay(1, 0, 320)
+        quant(1, 0)
+        for i in range(8):
+            nc.gpsimd.tensor_scalar(
+                out=rb[:, i, :], in0=br_bf[:], scalar1=r_f[:, i : i + 1], scalar2=0.0, op0=ALU.mult, op1=ALU.add
+            )
+        stage1(3, 0)
+        drain(1, 1)
+        lay(2, 0, 320)
+        quant(2, 0)
+        stage1(2, 1)
+        drain(3, 0)
+        lay(0, 1, 320)
+        quant(0, 1)
+        lay(3, 0, 320)
+        quant(3, 0)
+        drain(2, 1)
+        stage1(3, 1)
+        lay(1, 1, 320)
+        quant(1, 1)
+        for i in range(4):
+            for a in range(4):
+                s2(i, a, 4 + i)
+        lay(2, 1, 320)
+        quant(2, 1)
+        drain(3, 1)
+        for i in range(2):
+            finish(i)
+        for a in range(3):
+            for i in range(4, 6):
+                s2(i, a, i)
+        c_lay(3, 1, 0, 256, "v")
+        c_lay(3, 1, 256, 512, "s")
+        c_quant(3, 1, 0, 256)
+        for i in range(2, 4):
+            finish(i)
+        for a in range(3):
+            for i in range(6, 8):
+                s2(i, a, i)
+        c_quant(3, 1, 256, 512)
+        for i in range(4, 8):
+            s2(i, 3, None)
+            finish(i)

@@ -93,21 +93,21 @@ def tile_relu_dictionary_readout_s3_kernel(
         load_xr(0, 1, 2)
         load_er(0)
         load_xr(0, 2, 4)
+        load_eo(0)
+        load_xo(0)
+        load_xo(1)
         er_sc_v = er_scales.bitcast(I32)
         for q in range(4):
             nc.sync.dma_start(
                 out=er_sc_raw[32 * q : 32 * q + 4, :, :].bitcast(I32),
                 in_=er_sc_v[:, 4 * q : 4 * q + 4, :].rearrange("g q n -> q g n"),
             )
-        load_eo(0)
-        load_xo(0)
         load_eo(1)
         load_er(1)
         load_xr(1, 0, 2)
         load_xr(1, 2, 4)
         load_eo(2)
         load_er(2)
-        load_xo(1)
         load_eo(3)
         load_er(3)
         nc.sync.dma_start(out=d_codes[:], in_=d_words.rearrange("g p n -> p g n"))
@@ -143,11 +143,11 @@ def tile_relu_dictionary_readout_s3_kernel(
                     c = 128 * (2 * g + u)
                     nc.tensor.transpose(t[:, c : c + 128], words[:, 256 * g + u : 256 * (g + 1) : 2], ident[:])
 
-        def xr_product(i):
+        def xr_product(i, gs=(0, 1)):
             h = i // 4
             cols = slice(128 * (i % 4), 128 * (i % 4) + 128)
             t = xr_bank[i][:].bitcast(BF16)
-            for g in range(2):
+            for g in gs:
                 nc.vector.tensor_tensor(
                     out=x_in[h][1 + g][:, cols, :].rearrange("p m (u e) -> p m u e", u=2),
                     in0=t[:, 512 * g : 512 * (g + 1)].rearrange("p (u m e) -> p m u e", u=2, e=2),
@@ -212,7 +212,7 @@ def tile_relu_dictionary_readout_s3_kernel(
 
         def s1(a, h, t, c, first=0, last=2):
             if c == first:
-                s1_bank[a, h, t] = bank(t, "s1_%d_%d_%d" % (a, h, t))
+                s1_bank[a, h, t] = bank(len(s1_bank) % 6, "s1_%d_%d_%d" % (a, h, t))
             acc = s1_bank[a, h, t]
             cols = slice(128 * t, 128 * t + 128)
             if c == 0:
@@ -291,8 +291,8 @@ def tile_relu_dictionary_readout_s3_kernel(
                 for c in range(3):
                     s1(a, h, t, c)
 
-        def drain(a, h):
-            for t in range(4):
+        def drain(a, h, ts=(0, 1, 2, 3)):
+            for t in ts:
                 empty(a, h, t, "s")
 
         def lay(a, h, split):
@@ -304,23 +304,35 @@ def tile_relu_dictionary_readout_s3_kernel(
         def quant(a, h):
             c_quant(a, h, 0, 512)
 
+        def atoms(a):
+            er_move(a)
+            er_move_scales(a)
+            eo_quant(a)
+
+        SP = 384
+
         widen(0, "s")
         widen(1, "v")
         widen(2, "s")
         widen(3, "s")
         er_move(0)
         for i in range(4):
-            xr_turn(i, 4 + i)
-        xo_turn(0, 4)
-        xo_turn(1, 5)
+            xr_turn(i, (6, 7, 4, 5)[i])
+        xo_turn(0, 2)
+        xo_turn(1, 3)
+        xo_turn(2, 6)
+        xo_turn(3, 7)
         eo_lay(0, "g")
         for i in range(4):
             xr_product(i)
         xo_empty(0, "s")
         xo_empty(1, "s")
-        er_move_scales(0)
+        xo_empty(2, "s")
+        xo_empty(3, "s")
+        eo_lay(1, "s")
         x_quant(0, 1)
         x_quant(0, 2)
+        er_move_scales(0)
         for t in range(4):
             s1(0, 0, t, 1, 1, 0)
             s1(0, 0, t, 2, 1, 0)
@@ -328,89 +340,78 @@ def tile_relu_dictionary_readout_s3_kernel(
         eo_quant(0)
         for t in range(4):
             s1(0, 0, t, 0, 1, 0)
-        eo_lay(1, "g")
+        atoms(1)
         widen(4, "s")
+        drain(0, 0, (0, 1))
+        stage1(1, 0, (0,))
+        xr_turn(4, 6)
         widen(5, "s")
-        xr_turn(4, 4)
-        eo_quant(1)
-        er_move(1)
-        er_move_scales(1)
-        eo_lay(2, "g")
-        drain(0, 0)
-        stage1(1, 0)
-        xr_turn(5, 5)
-        widen(6, "s")
-        widen(7, "s")
+        drain(0, 0, (2, 3))
+        eo_lay(2, "v")
+        atoms(2)
         xr_product(4)
-        eo_quant(2)
-        er_move(2)
-        er_move_scales(2)
-        drain(1, 0)
+        stage1(1, 0, (1, 2))
+        xr_turn(5, 7)
+        stage1(1, 0, (3,))
+        widen(6, "s")
+        drain(1, 0, (0, 1))
+        widen(7, "s")
+        drain(1, 0, (2, 3))
         xr_product(5)
-        stage1(2, 0, (0, 1))
         xr_turn(6, 6)
+        stage1(2, 0, (0,))
         xr_turn(7, 7)
-        stage1(2, 0, (2,))
-        xo_turn(2, 4)
-        xo_turn(3, 5)
-        stage1(2, 0, (3,))
         xr_product(6)
         xr_product(7)
-        xo_empty(2, "s")
-        xo_empty(3, "s")
+        stage1(2, 0, (1, 2, 3))
         drain(2, 0)
+        x_quant(1, 0)
         x_quant(1, 1)
         x_quant(1, 2)
-        x_quant(1, 0)
-        eo_lay(3, "s")
-        lay(0, 0, 512)
+        lay(0, 0, SP)
         stage1(0, 1)
-        eo_quant(3)
         er_move(3)
         er_move_scales(3)
         quant(0, 0)
+        eo_lay(3, "v")
         stage1(1, 1)
         drain(0, 1)
-        lay(1, 0, 320)
+        lay(1, 0, SP)
+        eo_quant(3)
         quant(1, 0)
         for i in range(8):
             nc.gpsimd.tensor_scalar(
                 out=rb[:, i, :], in0=br_bf[:], scalar1=r_f[:, i : i + 1], scalar2=0.0, op0=ALU.mult, op1=ALU.add
             )
-        stage1(3, 0)
-        drain(1, 1)
-        lay(2, 0, 320)
-        quant(2, 0)
         stage1(2, 1)
-        drain(3, 0)
-        lay(0, 1, 320)
-        quant(0, 1)
-        lay(3, 0, 320)
-        quant(3, 0)
+        drain(1, 1)
+        lay(2, 0, SP)
+        quant(2, 0)
+        stage1(3, 0)
         drain(2, 1)
-        stage1(3, 1)
-        lay(1, 1, 320)
+        lay(0, 1, SP)
+        quant(0, 1)
+        lay(1, 1, SP)
         quant(1, 1)
+        drain(3, 0)
+        stage1(3, 1)
+        lay(3, 0, SP)
+        quant(3, 0)
+        lay(2, 1, SP)
+        drain(3, 1)
         for i in range(4):
             for a in range(4):
-                s2(i, a, 4 + i)
-        lay(2, 1, 320)
+                s2(i, a, (6, 7, 0, 1)[i])
         quant(2, 1)
-        drain(3, 1)
-        for i in range(2):
-            finish(i)
-        for a in range(3):
-            for i in range(4, 6):
-                s2(i, a, i)
+        finish(0)
         c_lay(3, 1, 0, 256, "v")
         c_lay(3, 1, 256, 512, "s")
         c_quant(3, 1, 0, 256)
-        for i in range(2, 4):
-            finish(i)
-        for a in range(3):
-            for i in range(6, 8):
-                s2(i, a, i)
+        finish(1)
         c_quant(3, 1, 256, 512)
+        finish(2)
+        finish(3)
         for i in range(4, 8):
-            s2(i, 3, None)
+            for a in range(4):
+                s2(i, a, i - 2)
             finish(i)

@@ -36,6 +36,7 @@ def tile_relu_dictionary_readout_s3_kernel(
         ident = kt([P, P], F32, "ident")
         er_sc_raw = kt([P, 2, F], U8, "er_sc_raw")
         d_sc = kt([P, 4, N], U8, "d_sc")
+        dummy = kt([P, 512], BF16, "dummy")
         warm = kt([P, 1], F32, "warm")
         xr_raw = [kt([P, 4, KR], U8, "xr_raw%d" % h) for h in range(2)]
         xr_wide = kt([P, 8, KR], BF16, "xr_wide")
@@ -68,13 +69,12 @@ def tile_relu_dictionary_readout_s3_kernel(
         out_v = out.rearrange("(p i) n -> p i n", i=8)
 
         nc.vector.memset(warm[:], 0.0)
+        nc.vector.memset(dummy[:], 0.0)
         make_identity(nc, ident[:])
         nc.gpsimd.memset(er_sc_raw[:].rearrange("p g n -> p (g n)").bitcast(I32), 0)
         nc.gpsimd.memset(d_sc[:].rearrange("p g n -> p (g n)").bitcast(I32), 0)
 
         nc.scalar.dma_start(out=xr_sc[:], in_=xr_scale.rearrange("o (g p t) -> p (o g) t", p=128, t=4))
-        nc.scalar.dma_start(out=b_bf[:], in_=b.rearrange("(a p t) -> p a t", p=128, t=4))
-        nc.scalar.dma_start(out=r_bf[:], in_=r.rearrange("(p i) -> p i", i=8))
         nc.scalar.activation(out=warm[:], in_=warm[:], func=ACT.Relu)
 
         def load_xr(h, lo, hi):
@@ -102,6 +102,8 @@ def tile_relu_dictionary_readout_s3_kernel(
                 out=er_sc_raw[32 * q : 32 * q + 4, :, :].bitcast(I32),
                 in_=er_sc_v[:, 4 * q : 4 * q + 4, :].rearrange("g q n -> q g n"),
             )
+        nc.sync.dma_start(out=b_bf[:], in_=b.rearrange("(a p t) -> p a t", p=128, t=4))
+        nc.sync.dma_start(out=r_bf[:], in_=r.rearrange("(p i) -> p i", i=8))
         load_eo(1)
         load_er(1)
         load_xr(1, 0, 2)
@@ -119,8 +121,17 @@ def tile_relu_dictionary_readout_s3_kernel(
             )
         nc.sync.dma_start(out=br_bf[:], in_=b_read.partition_broadcast(P))
 
-        nc.gpsimd.tensor_copy(out=b_f[:], in_=b_bf[:].rearrange("p a t -> p (a t)"))
-        nc.gpsimd.tensor_copy(out=r_f[:], in_=r_bf[:])
+        def cast_columns():
+            nc.gpsimd.tensor_copy(out=b_f[:], in_=b_bf[:].rearrange("p a t -> p (a t)"))
+            nc.gpsimd.tensor_copy(out=r_f[:], in_=r_bf[:])
+
+        def warm_up(k, n):
+            t = psum.tile([P, 512], F32, name="warm_bank", tag="bank%d" % k)
+            for i in range(n):
+                nc.tensor.matmul(out=t[:], lhsT=dummy[:, 0:128], rhs=dummy[:], start=True, stop=True)
+
+        def bias_row(i):
+            nc.vector.tensor_scalar(out=rb[:, i, :], in0=br_bf[:], scalar1=r_f[:, i : i + 1], scalar2=None, op0=ALU.mult)
 
         def bank(k, name):
             return psum.tile([P, 512], F32, name=name, tag="bank%d" % k)
@@ -196,11 +207,10 @@ def tile_relu_dictionary_readout_s3_kernel(
             nc.vector.quantize_mx(out=eo_codes[a][:].bitcast(E4), scales=eo_scales[a][:], in_=eo_in[a][:])
 
         def er_move(a):
-            for g in range(2):
-                nc.vector.tensor_copy(
-                    out=er_codes[a][:, g, :].rearrange("p (t m c) -> p t m c", t=4, c=2),
-                    in_=er_raw[a][:, g, :].rearrange("p (m t c) -> p t m c", t=4, c=2),
-                )
+            nc.vector.tensor_copy(
+                out=er_codes[a][:].rearrange("p g (t m c) -> p g t m c", t=4, c=2),
+                in_=er_raw[a][:].rearrange("p g (m t c) -> p g t m c", t=4, c=2),
+            )
 
         def er_move_scales(a):
             nc.vector.tensor_copy(
@@ -279,7 +289,7 @@ def tile_relu_dictionary_readout_s3_kernel(
             )
 
         def finish(i):
-            y = roll.tile([P, N], F32, name="y", tag="y", align_bytes=64)
+            y = roll.tile([P, N], F32, name="y", tag="y", bufs=8, align_bytes=64)
             nc.vector.scalar_tensor_tensor(
                 out=y[:], in0=s2_bank[i][:], scalar=r_f[:, i : i + 1], in1=rb[:, i, :], op0=ALU.mult, op1=ALU.add
             )
@@ -322,7 +332,9 @@ def tile_relu_dictionary_readout_s3_kernel(
         xo_turn(1, 3)
         xo_turn(2, 6)
         xo_turn(3, 7)
+        warm_up(5, 4)
         eo_lay(0, "g")
+        cast_columns()
         for i in range(4):
             xr_product(i)
         xo_empty(0, "s")
@@ -343,23 +355,22 @@ def tile_relu_dictionary_readout_s3_kernel(
         atoms(1)
         widen(4, "s")
         drain(0, 0, (0, 1))
-        stage1(1, 0, (0,))
-        xr_turn(4, 6)
+        stage1(1, 0, (0, 1))
         widen(5, "s")
+        xr_turn(4, 6)
+        xr_turn(5, 7)
         drain(0, 0, (2, 3))
         eo_lay(2, "v")
         atoms(2)
         xr_product(4)
-        stage1(1, 0, (1, 2))
-        xr_turn(5, 7)
-        stage1(1, 0, (3,))
+        stage1(1, 0, (2, 3))
         widen(6, "s")
         drain(1, 0, (0, 1))
         widen(7, "s")
         drain(1, 0, (2, 3))
         xr_product(5)
-        xr_turn(6, 6)
         stage1(2, 0, (0,))
+        xr_turn(6, 6)
         xr_turn(7, 7)
         xr_product(6)
         xr_product(7)
@@ -379,20 +390,20 @@ def tile_relu_dictionary_readout_s3_kernel(
         lay(1, 0, SP)
         eo_quant(3)
         quant(1, 0)
-        for i in range(8):
-            nc.gpsimd.tensor_scalar(
-                out=rb[:, i, :], in0=br_bf[:], scalar1=r_f[:, i : i + 1], scalar2=0.0, op0=ALU.mult, op1=ALU.add
-            )
         stage1(2, 1)
         drain(1, 1)
         lay(2, 0, SP)
         quant(2, 0)
+        for i in range(0, 4):
+            bias_row(i)
         stage1(3, 0)
         drain(2, 1)
         lay(0, 1, SP)
         quant(0, 1)
         lay(1, 1, SP)
         quant(1, 1)
+        for i in range(4, 8):
+            bias_row(i)
         drain(3, 0)
         stage1(3, 1)
         lay(3, 0, SP)

@@ -31,7 +31,7 @@ def tile_relu_dictionary_readout_s3_kernel(
         ctx.enter_context(tc.manual_schedule())
 
         def kt(shape, dt, name):
-            return keep.tile(shape, dt, name=name, tag=name, align_bytes=64)
+            return keep.tile(shape, dt, name=name, tag=name, align_bytes=256)
 
         ident = kt([P, P], F32, "ident")
         er_sc_raw = kt([P, 2, F], U8, "er_sc_raw")
@@ -46,7 +46,7 @@ def tile_relu_dictionary_readout_s3_kernel(
         x_codes = [[kt([P, 512], U32, "x_codes%d_%d" % (h, c)) for c in range(3)] for h in range(2)]
         x_scales = [[kt([P, 512], U8, "x_scales%d_%d" % (h, c)) for c in range(3)] for h in range(2)]
         eo_raw = [kt([P, 4, 512], BF16, "eo_raw%d" % a) for a in range(4)]
-        eo_in = [kt([P, 2048], BF16, "eo_in%d" % a) for a in range(4)]
+        eo_in = [kt([P, 2048], BF16, "eo_in%d" % a) for a in range(2)]
         eo_codes = [kt([P, 512], U32, "eo_codes%d" % a) for a in range(4)]
         eo_scales = [kt([P, 512], U8, "eo_scales%d" % a) for a in range(4)]
         er_raw = [kt([P, 2, 1024], U8, "er_raw%d" % a) for a in range(4)]
@@ -110,7 +110,6 @@ def tile_relu_dictionary_readout_s3_kernel(
         load_xr(1, 2, 4)
         load_eo(2)
         load_er(2)
-        load_eo(3)
         load_er(3)
         nc.sync.dma_start(out=d_codes[:], in_=d_words.rearrange("g p n -> p g n"))
         d_sc_v = d_scales.bitcast(I32)
@@ -120,6 +119,7 @@ def tile_relu_dictionary_readout_s3_kernel(
                 in_=d_sc_v[:, 4 * q : 4 * q + 4, :].rearrange("g q n -> q g n"),
             )
         nc.sync.dma_start(out=br_bf[:], in_=b_read.partition_broadcast(P))
+        load_eo(3)
 
         def cast_columns():
             nc.gpsimd.tensor_copy(out=b_f[:], in_=b_bf[:].rearrange("p a t -> p (a t)"))
@@ -194,7 +194,7 @@ def tile_relu_dictionary_readout_s3_kernel(
             )
 
         def eo_lay(a, eng):
-            o = eo_in[a][:].rearrange("p (t m j) -> p t m j", t=4, j=4)
+            o = eo_in[a % 2][:].rearrange("p (t m j) -> p t m j", t=4, j=4)
             s = eo_raw[a][:].rearrange("p j (m t) -> p t m j", t=4)
             if eng == "s":
                 nc.scalar.copy(out=o, in_=s)
@@ -204,7 +204,7 @@ def tile_relu_dictionary_readout_s3_kernel(
                 nc.vector.tensor_copy(out=o, in_=s)
 
         def eo_quant(a):
-            nc.vector.quantize_mx(out=eo_codes[a][:].bitcast(E4), scales=eo_scales[a][:], in_=eo_in[a][:])
+            nc.vector.quantize_mx(out=eo_codes[a][:].bitcast(E4), scales=eo_scales[a][:], in_=eo_in[a % 2][:])
 
         def er_move(a):
             nc.vector.tensor_copy(
@@ -243,7 +243,7 @@ def tile_relu_dictionary_readout_s3_kernel(
 
         def empty(a, h, t, eng):
             if t == 0:
-                c_act[a, h] = roll.tile([P, 4, 512], BF16, name="c_act", tag="c_act", align_bytes=64)
+                c_act[a, h] = roll.tile([P, 4, 512], BF16, name="c_act", tag="c_act", align_bytes=256)
             o = c_act[a, h][:, t, :]
             s = s1_bank[a, h, t][:]
             bias = b_f[:, 4 * a + t : 4 * a + t + 1]
@@ -256,7 +256,7 @@ def tile_relu_dictionary_readout_s3_kernel(
 
         def c_lay(a, h, lo, hi, eng):
             if lo == 0:
-                c_in[a, h] = roll.tile([P, 512, 4], BF16, name="c_in", tag="c_in", align_bytes=64)
+                c_in[a, h] = roll.tile([P, 512, 4], BF16, name="c_in", tag="c_in", align_bytes=256)
             o = c_in[a, h][:, lo:hi, :]
             s = c_act[a, h][:, :, lo:hi].rearrange("p t m -> p m t")
             if eng == "s":
@@ -289,7 +289,7 @@ def tile_relu_dictionary_readout_s3_kernel(
             )
 
         def finish(i):
-            y = roll.tile([P, N], F32, name="y", tag="y", bufs=8, align_bytes=64)
+            y = roll.tile([P, N], F32, name="y", tag="y", bufs=6, align_bytes=256)
             nc.vector.scalar_tensor_tensor(
                 out=y[:], in0=s2_bank[i][:], scalar=r_f[:, i : i + 1], in1=rb[:, i, :], op0=ALU.mult, op1=ALU.add
             )
@@ -319,7 +319,7 @@ def tile_relu_dictionary_readout_s3_kernel(
             er_move_scales(a)
             eo_quant(a)
 
-        SP = 384
+        SP = 448
 
         widen(0, "s")
         widen(1, "v")
@@ -372,6 +372,7 @@ def tile_relu_dictionary_readout_s3_kernel(
         stage1(2, 0, (0,))
         xr_turn(6, 6)
         xr_turn(7, 7)
+        eo_lay(3, "g")
         xr_product(6)
         xr_product(7)
         stage1(2, 0, (1, 2, 3))
@@ -384,7 +385,6 @@ def tile_relu_dictionary_readout_s3_kernel(
         er_move(3)
         er_move_scales(3)
         quant(0, 0)
-        eo_lay(3, "v")
         stage1(1, 1)
         drain(0, 1)
         lay(1, 0, SP)

from contextlib import ExitStack

import concourse.mybir as mybir
from concourse.masks import make_identity

M, KO, KR, F, N = 1024, 512, 1024, 2048, 512
FLOPS = 2 * M * F * (KO + KR) + 2 * M * F * N

F32 = mybir.dt.float32
BF16 = mybir.dt.bfloat16
I32 = mybir.dt.int32
U32 = mybir.dt.uint32
U8 = mybir.dt.uint8
E4 = mybir.dt.float8_e4m3fn_x4
E2 = mybir.dt.float4_e2m1fn_x4
FP8 = mybir.dt.float8_e4m3fn
ACT = mybir.ActivationFunctionType
ALU = mybir.AluOpType

P = 128


def tile_relu_dictionary_readout_s3_kernel(
    tc, xo, xr_bytes, xr_scale, eo, er_words, er_scales, b, d_words, d_scales, b_read, r, out
):
    nc = tc.nc
    with ExitStack() as ctx:
        keep = ctx.enter_context(tc.tile_pool(name="keep", bufs=1))
        roll = ctx.enter_context(tc.tile_pool(name="roll", bufs=4))
        psum = ctx.enter_context(tc.psum_pool(name="psum", bufs=1))
        ctx.enter_context(tc.manual_schedule())

        def kt(shape, dt, name):
            return keep.tile(shape, dt, name=name, tag=name, align_bytes=256)

        ident = kt([P, P], F32, "ident")
        er_sc_raw = kt([P, 2, F], U8, "er_sc_raw")
        d_sc = kt([P, 4, N], U8, "d_sc")
        dummy = kt([P, 512], BF16, "dummy")
        warm = kt([P, 1], F32, "warm")
        xr_raw = [kt([P, 4, KR], U8, "xr_raw%d" % h) for h in range(2)]
        xr_wide = kt([P, 8, KR], BF16, "xr_wide")
        xo_raw = [kt([P, 4, KO], BF16, "xo_raw%d" % h) for h in range(2)]
        xr_sc = kt([P, 2, 4], F32, "xr_sc")
        x_in = [[kt([P, 512, 4], BF16, "x_in%d_%d" % (h, c)) for c in range(3)] for h in range(2)]
        x_codes = [[kt([P, 512], U32, "x_codes%d_%d" % (h, c)) for c in range(3)] for h in range(2)]
        x_scales = [[kt([P, 512], U8, "x_scales%d_%d" % (h, c)) for c in range(3)] for h in range(2)]
        eo_raw = [kt([P, 4, 512], BF16, "eo_raw%d" % a) for a in range(4)]
        eo_in = [kt([P, 2048], BF16, "eo_in%d" % a) for a in range(2)]
        eo_codes = [kt([P, 512], U32, "eo_codes%d" % a) for a in range(4)]
        eo_scales = [kt([P, 512], U8, "eo_scales%d" % a) for a in range(4)]
        er_raw = [kt([P, 2, 1024], U8, "er_raw%d" % a) for a in range(4)]
        er_codes = [kt([P, 2, 1024], U8, "er_codes%d" % a) for a in range(4)]
        er_sc = [kt([P, 2, 512], U8, "er_sc%d" % a) for a in range(4)]
        d_codes = kt([P, 4, 2 * N], U8, "d_codes")
        c_codes = [[kt([P, 512], U32, "c_codes%d_%d" % (a, h)) for h in range(2)] for a in range(4)]
        c_scales = [[kt([P, 512], U8, "c_scales%d_%d" % (a, h)) for h in range(2)] for a in range(4)]
        b_bf = kt([P, 4, 4], BF16, "b_bf")
        b_f = kt([P, 16], F32, "b_f")
        r_bf = kt([P, 8], BF16, "r_bf")
        r_f = kt([P, 8], F32, "r_f")
        br_bf = kt([P, N], BF16, "br_bf")
        rb = kt([P, 8, N], F32, "rb")

        xo_v = xo.rearrange("(p i) k -> p i k", i=8)
        xr_v = xr_bytes.rearrange("(p i) k -> p i k", i=8)
        eo_v = eo.rearrange("(p j) f -> p j f", j=4)
        er_v = er_words.rearrange("g p n -> p g n")
        out_v = out.rearrange("(p i) n -> p i n", i=8)

        nc.vector.memset(warm[:], 0.0)
        nc.vector.memset(dummy[:], 0.0)
        make_identity(nc, ident[:])
        nc.gpsimd.memset(er_sc_raw[:].rearrange("p g n -> p (g n)").bitcast(I32), 0)
        nc.gpsimd.memset(d_sc[:].rearrange("p g n -> p (g n)").bitcast(I32), 0)

        nc.scalar.dma_start(out=xr_sc[:], in_=xr_scale.rearrange("o (g p t) -> p (o g) t", p=128, t=4))
        nc.scalar.activation(out=warm[:], in_=warm[:], func=ACT.Relu)

        def load_xr(h, lo, hi):
            nc.sync.dma_start(out=xr_raw[h][:, lo:hi, :], in_=xr_v[:, 4 * h + lo : 4 * h + hi, :])

        def load_xo(h):
            nc.sync.dma_start(out=xo_raw[h][:], in_=xo_v[:, 4 * h : 4 * h + 4, :])

        def load_eo(a):
            nc.sync.dma_start(out=eo_raw[a][:], in_=eo_v[:, :, 512 * a : 512 * a + 512])

        def load_er(a):
            nc.sync.dma_start(out=er_raw[a][:], in_=er_v[:, :, 1024 * a : 1024 * a + 1024])

        load_xr(0, 0, 1)
        load_xr(0, 1, 2)
        load_er(0)
        load_xr(0, 2, 4)
        load_eo(0)
        load_xo(0)
        load_xo(1)
        er_sc_v = er_scales.bitcast(I32)
        for q in range(4):
            nc.sync.dma_start(
                out=er_sc_raw[32 * q : 32 * q + 4, :, :].bitcast(I32),
                in_=er_sc_v[:, 4 * q : 4 * q + 4, :].rearrange("g q n -> q g n"),
            )
        nc.sync.dma_start(out=b_bf[:], in_=b.rearrange("(a p t) -> p a t", p=128, t=4))
        nc.sync.dma_start(out=r_bf[:], in_=r.rearrange("(p i) -> p i", i=8))
        load_eo(1)
        load_er(1)
        load_xr(1, 0, 2)
        load_xr(1, 2, 4)
        load_eo(2)
        load_er(2)
        load_er(3)
        nc.sync.dma_start(out=d_codes[:], in_=d_words.rearrange("g p n -> p g n"))
        d_sc_v = d_scales.bitcast(I32)
        for q in range(4):
            nc.sync.dma_start(
                out=d_sc[32 * q : 32 * q + 4, :, :].bitcast(I32),
                in_=d_sc_v[:, 4 * q : 4 * q + 4, :].rearrange("g q n -> q g n"),
            )
        nc.sync.dma_start(out=br_bf[:], in_=b_read.partition_broadcast(P))
        load_eo(3)

        def cast_columns():
            nc.gpsimd.tensor_copy(out=b_f[:], in_=b_bf[:].rearrange("p a t -> p (a t)"))
            nc.gpsimd.tensor_copy(out=r_f[:], in_=r_bf[:])

        def warm_up(k, n):
            t = psum.tile([P, 512], F32, name="warm_bank", tag="bank%d" % k)
            for i in range(n):
                nc.tensor.matmul(out=t[:], lhsT=dummy[:, 0:128], rhs=dummy[:], start=True, stop=True)

        def bias_row(i):
            nc.vector.tensor_scalar(out=rb[:, i, :], in0=br_bf[:], scalar1=r_f[:, i : i + 1], scalar2=None, op0=ALU.mult)

        def bank(k, name):
            return psum.tile([P, 512], F32, name=name, tag="bank%d" % k)

        def widen(i, eng):
            src = xr_raw[i // 4][:, i % 4, :].bitcast(FP8)
            if eng == "s":
                nc.scalar.activation(out=xr_wide[:, i, :], in_=src, func=ACT.Copy)
            else:
                nc.vector.tensor_copy(out=xr_wide[:, i, :], in_=src)

        xr_bank = {}

        def xr_turn(i, k):
            t = bank(k, "xr_t%d" % i)
            xr_bank[i] = t
            words = xr_wide[:, i, :].bitcast(F32)
            for g in range(2):
                for u in range(2):
                    c = 128 * (2 * g + u)
                    nc.tensor.transpose(t[:, c : c + 128], words[:, 256 * g + u : 256 * (g + 1) : 2], ident[:])

        def xr_product(i, gs=(0, 1)):
            h = i // 4
            cols = slice(128 * (i % 4), 128 * (i % 4) + 128)
            t = xr_bank[i][:].bitcast(BF16)
            for g in gs:
                nc.vector.tensor_tensor(
                    out=x_in[h][1 + g][:, cols, :].rearrange("p m (u e) -> p m u e", u=2),
                    in0=t[:, 512 * g : 512 * (g + 1)].rearrange("p (u m e) -> p m u e", u=2, e=2),
                    in1=xr_sc[:, g, :].rearrange("p (u e) -> p u e", u=2).unsqueeze(1).to_broadcast([P, 128, 2, 2]),
                    op=ALU.mult,
                )

        xo_bank = {}

        def xo_turn(j, k):
            t = bank(k, "xo_t%d" % j)
            xo_bank[j] = t
            for d in range(2):
                i = 2 * j + d
                words = xo_raw[i // 4][:, i % 4, :].bitcast(F32)
                for u in range(2):
                    c = 128 * (2 * d + u)
                    nc.tensor.transpose(t[:, c : c + 128], words[:, u:256:2], ident[:])

        def xo_empty(j, eng):
            h = j // 2
            dst = x_in[h][0][:, 256 * (j % 2) : 256 * (j % 2) + 256, :].rearrange("p m t -> p (m t)").bitcast(F32)
            o = dst.rearrange("p (d m u) -> p d m u", d=2, u=2)
            s = xo_bank[j][:].rearrange("p (d u m) -> p d m u", d=2, u=2)
            if eng == "s":
                nc.scalar.copy(out=o, in_=s)
            else:
                nc.vector.tensor_copy(out=o, in_=s)

        def x_quant(h, c):
            nc.vector.quantize_mx(
                out=x_codes[h][c][:].bitcast(E4), scales=x_scales[h][c][:], in_=x_in[h][c][:].rearrange("p m t -> p (m t)")
            )

        def eo_lay(a, eng):
            o = eo_in[a % 2][:].rearrange("p (t m j) -> p t m j", t=4, j=4)
            s = eo_raw[a][:].rearrange("p j (m t) -> p t m j", t=4)
            if eng == "s":
                nc.scalar.copy(out=o, in_=s)
            elif eng == "g":
                nc.gpsimd.tensor_scalar(out=o, in0=s, scalar1=1.0, scalar2=0.0, op0=ALU.mult, op1=ALU.add)
            else:
                nc.vector.tensor_copy(out=o, in_=s)

        def eo_quant(a):
            nc.vector.quantize_mx(out=eo_codes[a][:].bitcast(E4), scales=eo_scales[a][:], in_=eo_in[a % 2][:])

        def er_move(a):
            nc.vector.tensor_copy(
                out=er_codes[a][:].rearrange("p g (t m c) -> p g t m c", t=4, c=2),
                in_=er_raw[a][:].rearrange("p g (m t c) -> p g t m c", t=4, c=2),
            )

        def er_move_scales(a):
            nc.vector.tensor_copy(
                out=er_sc[a][:].rearrange("p g (t m) -> p g t m", t=4),
                in_=er_sc_raw[:, :, 512 * a : 512 * a + 512].rearrange("p g (m t) -> p g t m", t=4),
            )

        s1_bank = {}

        def s1(a, h, t, c, first=0, last=2):
            if c == first:
                s1_bank[a, h, t] = bank(len(s1_bank) % 6, "s1_%d_%d_%d" % (a, h, t))
            acc = s1_bank[a, h, t]
            cols = slice(128 * t, 128 * t + 128)
            if c == 0:
                w, ws = eo_codes[a][:, cols].bitcast(E4), eo_scales[a][:, cols]
            else:
                w, ws = er_codes[a][:, c - 1, 256 * t : 256 * t + 256].bitcast(E2), er_sc[a][:, c - 1, cols]
            nc.tensor.matmul_mx(
                out=acc[:],
                lhsT=w,
                lhsT_scale=ws,
                rhs=x_codes[h][c][:].bitcast(E4),
                rhs_scale=x_scales[h][c][:],
                start=(c == first),
                stop=(c == last),
            )

        c_act = {}

        def empty(a, h, t, eng):
            if t == 0:
                c_act[a, h] = roll.tile([P, 4, 512], BF16, name="c_act", tag="c_act", align_bytes=256)
            o = c_act[a, h][:, t, :]
            s = s1_bank[a, h, t][:]
            bias = b_f[:, 4 * a + t : 4 * a + t + 1]
            if eng == "s":
                nc.scalar.activation(out=o, in_=s, func=ACT.Relu, bias=bias)
            else:
                nc.vector.tensor_scalar(out=o, in0=s, scalar1=bias, scalar2=0.0, op0=ALU.add, op1=ALU.max)

        c_in = {}

        def c_lay(a, h, lo, hi, eng):
            if lo == 0:
                c_in[a, h] = roll.tile([P, 512, 4], BF16, name="c_in", tag="c_in", align_bytes=256)
            o = c_in[a, h][:, lo:hi, :]
            s = c_act[a, h][:, :, lo:hi].rearrange("p t m -> p m t")
            if eng == "s":
                nc.scalar.copy(out=o, in_=s)
            else:
                nc.vector.tensor_copy(out=o, in_=s)

        def c_quant(a, h, lo, hi):
            nc.vector.quantize_mx(
                out=c_codes[a][h][:, lo:hi].bitcast(E4),
                scales=c_scales[a][h][:, lo:hi],
                in_=c_in[a, h][:, lo:hi, :].rearrange("p m t -> p (m t)"),
            )

        s2_bank = {}

        def s2(i, a, k):
            if a == 0:
                s2_bank[i] = bank(k, "s2_%d" % i)
            h = i // 4
            cols = slice(128 * (i % 4), 128 * (i % 4) + 128)
            nc.tensor.matmul_mx(
                out=s2_bank[i][:],
                lhsT=c_codes[a][h][:, cols].bitcast(E4),
                lhsT_scale=c_scales[a][h][:, cols],
                rhs=d_codes[:, a, :].bitcast(E2),
                rhs_scale=d_sc[:, a, :],
                start=(a == 0),
                stop=(a == 3),
            )

        def finish(i):
            y = roll.tile([P, N], F32, name="y", tag="y", bufs=6, align_bytes=256)
            nc.vector.scalar_tensor_tensor(
                out=y[:], in0=s2_bank[i][:], scalar=r_f[:, i : i + 1], in1=rb[:, i, :], op0=ALU.mult, op1=ALU.add
            )
            nc.sync.dma_start(out=out_v[:, i, :], in_=y[:])


        def stage1(a, h, ts=(0, 1, 2, 3)):
            for t in ts:
                for c in range(3):
                    s1(a, h, t, c)

        def drain(a, h, ts=(0, 1, 2, 3)):
            for t in ts:
                empty(a, h, t, "s")

        def lay(a, h, split):
            if split > 0:
                c_lay(a, h, 0, split, "v")
            if split < 512:
                c_lay(a, h, split, 512, "s")

        def quant(a, h):
            c_quant(a, h, 0, 512)

        def atoms(a):
            er_move(a)
            er_move_scales(a)
            eo_quant(a)

        SP = 448

        widen(0, "s")
        widen(1, "v")
        widen(2, "s")
        widen(3, "s")
        er_move(0)
        for i in range(4):
            xr_turn(i, (6, 7, 4, 5)[i])
        xo_turn(0, 2)
        xo_turn(1, 3)
        xo_turn(2, 6)
        xo_turn(3, 7)
        warm_up(5, 4)
        eo_lay(0, "g")
        cast_columns()
        for i in range(4):
            xr_product(i)
        xo_empty(0, "s")
        xo_empty(1, "s")
        xo_empty(2, "s")
        xo_empty(3, "s")
        eo_lay(1, "s")
        x_quant(0, 1)
        x_quant(0, 2)
        er_move_scales(0)
        for t in range(4):
            s1(0, 0, t, 1, 1, 0)
            s1(0, 0, t, 2, 1, 0)
        x_quant(0, 0)
        eo_quant(0)
        for t in range(4):
            s1(0, 0, t, 0, 1, 0)
        atoms(1)
        widen(4, "s")
        drain(0, 0, (0, 1))
        stage1(1, 0, (0, 1))
        widen(5, "s")
        xr_turn(4, 6)
        xr_turn(5, 7)
        drain(0, 0, (2, 3))
        eo_lay(2, "v")
        atoms(2)
        xr_product(4)
        stage1(1, 0, (2, 3))
        widen(6, "s")
        drain(1, 0, (0, 1))
        widen(7, "s")
        drain(1, 0, (2, 3))
        xr_product(5)
        stage1(2, 0, (0,))
        xr_turn(6, 6)
        xr_turn(7, 7)
        eo_lay(3, "g")
        xr_product(6)
        xr_product(7)
        stage1(2, 0, (1, 2, 3))
        drain(2, 0)
        x_quant(1, 0)
        x_quant(1, 1)
        x_quant(1, 2)
        lay(0, 0, SP)
        stage1(0, 1)
        er_move(3)
        er_move_scales(3)
        quant(0, 0)
        stage1(1, 1)
        drain(0, 1)
        lay(1, 0, SP)
        eo_quant(3)
        quant(1, 0)
        stage1(2, 1)
        drain(1, 1)
        lay(2, 0, SP)
        quant(2, 0)
        for i in range(0, 4):
            bias_row(i)
        stage1(3, 0)
        drain(2, 1)
        lay(0, 1, SP)
        quant(0, 1)
        lay(1, 1, SP)
        quant(1, 1)
        for i in range(4, 8):
            bias_row(i)
        drain(3, 0)
        stage1(3, 1)
        lay(3, 0, SP)
        quant(3, 0)
        lay(2, 1, SP)
        drain(3, 1)
        for i in range(4):
            for a in range(4):
                s2(i, a, (6, 7, 0, 1)[i])
        quant(2, 1)
        finish(0)
        c_lay(3, 1, 0, 256, "v")
        c_lay(3, 1, 256, 512, "s")
        c_quant(3, 1, 0, 256)
        finish(1)
        c_quant(3, 1, 256, 512)
        finish(2)
        finish(3)
        for i in range(4, 8):
            for a in range(4):
                s2(i, a, i - 2)
            finish(i)
